import numpy as np, ml_dtypes
CORES = [16,17,18,19,20,21,22,23,32,33,34,35,36,37,38,39,48,49,50,51,52,53,54,55]
N = 24
TOK = 32
EXPERTS = [2,4,5,6,12,14,15,21]
ROUTE = [[[5],[15],[15],[14],[5],[12],[4],[21],[5],[14],[21],[21],[5],[2],[14],[15],[21],[4],[21],[2],[6],[14],[21],[2],[6],[2],[5],[4],[15],[12],[14],[6]],[[6],[12],[12],[6],[15],[2],[5],[12],[21],[4],[12],[12],[21],[12],[21],[6],[6],[12],[6],[6],[2],[4],[14],[4],[21],[21],[6],[12],[4],[4],[5],[12]],[[5],[6],[5],[5],[6],[12],[15],[21],[21],[14],[12],[6],[6],[6],[15],[21],[14],[12],[12],[5],[12],[2],[2],[12],[6],[4],[15],[14],[6],[6],[15],[15]],[[12],[21],[15],[4],[4],[14],[14],[4],[12],[14],[12],[12],[15],[12],[21],[4],[2],[15],[21],[6],[14],[5],[21],[12],[5],[12],[6],[6],[5],[2],[15],[4]],[[6],[12],[5],[4],[5],[21],[4],[4],[4],[2],[5],[5],[21],[12],[14],[15],[5],[2],[2],[14],[6],[5],[6],[4],[6],[21],[6],[12],[6],[2],[2],[5]],[[4],[5],[6],[21],[21],[4],[4],[6],[6],[15],[12],[6],[15],[5],[6],[15],[2],[5],[14],[21],[6],[14],[21],[12],[5],[15],[2],[2],[12],[6],[14],[14]],[[21],[12],[15],[6],[14],[2],[15],[12],[2],[5],[6],[5],[14],[2],[6],[4],[14],[6],[12],[21],[6],[6],[21],[5],[12],[15],[4],[21],[15],[15],[12],[2]],[[2],[14],[4],[15],[21],[5],[6],[2],[14],[12],[21],[6],[14],[15],[6],[5],[14],[2],[6],[6],[14],[6],[12],[14],[21],[6],[5],[15],[14],[6],[5],[4]],[[14],[6],[5],[14],[14],[15],[12],[6],[4],[21],[15],[12],[15],[12],[12],[15],[21],[6],[4],[2],[4],[21],[21],[5],[6],[12],[15],[14],[14],[12],[21],[6]],[[15],[12],[14],[6],[12],[15],[21],[2],[5],[5],[6],[4],[5],[15],[4],[12],[4],[21],[12],[6],[6],[12],[14],[15],[6],[21],[15],[12],[21],[21],[12],[6]],[[14],[4],[21],[14],[2],[4],[14],[21],[14],[12],[4],[6],[4],[15],[4],[6],[2],[21],[15],[21],[2],[6],[12],[4],[14],[2],[12],[5],[5],[6],[6],[6]],[[5],[21],[15],[4],[5],[12],[6],[4],[4],[14],[12],[4],[14],[6],[14],[5],[4],[12],[5],[6],[21],[5],[5],[2],[15],[5],[21],[12],[15],[12],[5],[5]],[[4],[5],[12],[12],[4],[14],[6],[4],[5],[15],[21],[14],[2],[21],[15],[5],[5],[5],[14],[5],[6],[21],[21],[6],[6],[6],[15],[4],[15],[6],[2],[2]],[[21],[12],[4],[15],[5],[12],[12],[4],[5],[6],[4],[21],[5],[5],[6],[6],[14],[12],[6],[21],[2],[12],[15],[6],[5],[6],[15],[6],[12],[4],[2],[2]],[[15],[14],[6],[4],[12],[21],[4],[21],[14],[4],[15],[5],[5],[5],[5],[15],[21],[21],[6],[5],[4],[6],[5],[4],[21],[14],[14],[6],[5],[5],[15],[4]],[[4],[5],[6],[21],[14],[2],[12],[4],[5],[4],[4],[21],[5],[14],[12],[6],[15],[5],[2],[12],[21],[4],[21],[6],[4],[5],[21],[14],[6],[6],[14],[6]],[[14],[15],[6],[15],[6],[15],[12],[21],[15],[6],[6],[15],[21],[15],[14],[6],[21],[12],[2],[12],[4],[14],[15],[5],[15],[21],[6],[15],[2],[4],[4],[21]],[[5],[21],[4],[2],[14],[15],[14],[21],[4],[6],[5],[14],[14],[12],[2],[6],[5],[14],[6],[21],[15],[12],[4],[21],[14],[2],[6],[4],[2],[21],[2],[21]],[[6],[2],[15],[12],[2],[12],[5],[6],[5],[14],[2],[2],[15],[6],[21],[2],[6],[15],[12],[21],[15],[5],[12],[6],[14],[12],[21],[5],[14],[14],[21],[6]],[[21],[12],[14],[15],[5],[14],[21],[5],[6],[6],[12],[14],[5],[4],[12],[14],[14],[21],[15],[14],[2],[5],[2],[12],[12],[15],[2],[14],[5],[6],[14],[15]],[[21],[6],[15],[14],[14],[14],[5],[15],[5],[14],[12],[6],[5],[12],[6],[15],[6],[6],[14],[15],[14],[12],[4],[21],[2],[4],[15],[15],[14],[2],[15],[6]],[[2],[5],[5],[4],[15],[21],[14],[4],[2],[15],[12],[5],[12],[6],[14],[2],[6],[15],[5],[4],[2],[21],[15],[15],[14],[12],[12],[6],[21],[4],[21],[4]],[[21],[6],[6],[14],[15],[4],[6],[21],[14],[2],[14],[14],[15],[2],[12],[4],[15],[21],[21],[4],[15],[5],[6],[2],[15],[21],[6],[14],[15],[5],[5],[14]],[[6],[4],[15],[4],[12],[4],[14],[2],[6],[21],[2],[2],[15],[5],[14],[21],[6],[4],[15],[12],[5],[21],[21],[6],[21],[15],[2],[4],[5],[4],[5],[2]]]
def setup_inputs(rng):
    return {"x": rng.standard_normal((N, 128, TOK), dtype=np.float32).astype(ml_dtypes.bfloat16), "w": rng.standard_normal((N, 128, 128), dtype=np.float32).astype(ml_dtypes.bfloat16)}
def reference(x, w):
    X, W = x.astype(np.float64), w.astype(np.float64)
    y = np.zeros((N, 128, TOK))
    for r in range(N):
        for t in range(TOK):
            for e in ROUTE[r][t]:
                y[r][:, t] += W[e].T @ X[r][:, t]
    return {"y": y.astype(ml_dtypes.bfloat16 if x.dtype != np.float64 else np.float64)}

@@ -1,0 +1,140 @@
+from concourse.bass import DstId, RemoteDMATransfer
+from concourse.mybir import AluOpType
+
+NE = 8
+TOK = 32
+D = 128
+
+SCRATCH = {
+    "wd": ("dram", [D, D], "bfloat16"),
+    "W": ("sbuf", [D, NE * D], "bfloat16"),
+    "xs": ("sbuf", [D, TOK], "bfloat16"),
+    "mask": ("sbuf", [D, NE * TOK], "bfloat16"),
+    "xm": ("sbuf", [D, NE * TOK], "bfloat16"),
+    "acc": ("psum", [D, TOK], "float32"),
+    "ys": ("sbuf", [D, TOK], "bfloat16"),
+}
+SEMAPHORES = ["ld", "h1", "sent", "xl", "mk", "xr", "mm", "cp", "st"] + ["ws%d" % j for j in range(NE)]
+
+
+def _bits(m):
+    return bin(m).count("1")
+
+
+def _plan(T, topo):
+    cores = list(T.cores)
+    experts = list(T.tables["EXPERTS"])
+    route = T.tables["ROUTE"]
+    slot = {e: j for j, e in enumerate(experts)}
+    home = [cores[e] for e in experts]
+    need = {c: sorted({slot[e] for tok in route[r] for e in tok}) for r, c in enumerate(cores)}
+    chips = sorted({topo.chip(c) for c in cores})
+    spread = {}
+    for ch in chips:
+        mem = [c for c in cores if topo.chip(c) == ch]
+        free = [c for c in mem if c not in home]
+        foreign = []
+        for j, h in enumerate(home):
+            if topo.chip(h) == ch:
+                spread[(ch, j)] = h
+            elif any(j in need[c] for c in mem):
+                foreign.append(j)
+        for same_die in (True, False):
+            for j in foreign:
+                if (ch, j) in spread:
+                    continue
+                for c in free:
+                    if topo.may_write(home[j], c) and (not same_die or topo.die(c) == topo.die(home[j])):
+                        spread[(ch, j)] = c
+                        free.remove(c)
+                        break
+    return cores, home, need, chips, spread
+
+
+def _send(g, topo, core, dsts, src, dst, rsem, lsem):
+    m = topo.mask(core, dsts[0])
+    for d in dsts:
+        m &= topo.mask(core, d)
+    ids = [DstId(rid=topo.addr(d)[0], pnc=topo.addr(d)[1]) for d in dsts]
+    g.remote_dma_fused(
+        [RemoteDMATransfer(dst_ids=ids, dma_engine_mask=m, remote_sem=rsem, srcs=[src], dsts=[dst for _ in dsts])],
+        local_sem=lsem)
+    return _bits(m)
+
+
+def rank_program(g, core, T, topo):
+    rank = T.rank_of(core)
+    if rank is None:
+        return
+    S = T.sem
+    cores, home, need, chips, spread = _plan(T, topo)
+    ch = topo.chip(core)
+    mine = [j for j in range(NE) if spread.get((ch, j)) == core]
+    my = mine[0] if mine else None
+    is_home = my is not None and home[my] == core
+    wants = need[core]
+
+    def wblk(j):
+        return T.W[:, j * D:(j + 1) * D]
+
+    def xblk(t, j):
+        return t[:, j * TOK:(j + 1) * TOK]
+
+    if is_home:
+        g.sync.dma_start(T.wd[:], T.w[:]).then_inc(S.ld, 16)
+    g.scalar.dma_start(T.xs[:], T.x[:]).then_inc(S.xl, 16)
+    if is_home and my in wants:
+        g.scalar.dma_start(wblk(my), T.w[:]).then_inc(S["ws%d" % my], 16)
+
+    sent = 0
+    if my is not None:
+        near = [c for c in cores if topo.chip(c) == ch and c != core and my in need[c]]
+        if is_home:
+            g.wait_ge(S.ld, 16)
+            far = [spread[(k, my)] for k in chips if k != ch and (k, my) in spread]
+            if far:
+                sent += _send(g, topo, core, far, T.wd[:], T.wd[:], S.h1, S.sent)
+        else:
+            n_in = _bits(topo.mask(home[my], core))
+            g.wait_ge(S.h1, n_in)
+            if my in wants:
+                g.sync.wait_ge(S.h1, n_in)
+                g.sync.dma_start(wblk(my), T.wd[:]).then_inc(S["ws%d" % my], 16)
+        if near:
+            sent += _send(g, topo, core, near, T.wd[:], wblk(my), S["ws%d" % my], S.sent)
+    if sent:
+        g.wait_ge(S.sent, sent)
+
+    v = g.vector
+    v.memset(T.mask[:], 0.0).then_inc(S.mk, 1)
+    v.wait_ge(S.mk, 1)
+    nmk = 1
+    experts = list(T.tables["EXPERTS"])
+    cols = sorted(experts.index(e) * TOK + t for t, tok in enumerate(T.tables["ROUTE"][rank]) for e in tok)
+    i = 0
+    while i < len(cols):
+        k = i
+        while k + 1 < len(cols) and cols[k + 1] == cols[k] + 1:
+            k += 1
+        v.memset(T.mask[:, cols[i]:cols[k] + 1], 1.0).then_inc(S.mk, 1)
+        nmk += 1
+        i = k + 1
+    v.wait_ge(S.mk, nmk)
+    v.wait_ge(S.xl, 16)
+    for j in wants:
+        v.tensor_tensor(xblk(T.xm, j), T.xs[:], xblk(T.mask, j), AluOpType.mult).then_inc(S.xr, 1)
+
+    t = g.tensor
+    t.wait_ge(S.xr, len(wants))
+    order = sorted(wants, key=lambda j: (topo.chip(home[j]) != ch, j != my, j))
+    for i, j in enumerate(order):
+        src = spread[(ch, j)]
+        t.wait_ge(S["ws%d" % j], 16 if src == core else _bits(topo.mask(src, core)))
+        mm = t.matmul(T.acc[:], wblk(j), xblk(T.xm, j), start=(i == 0), stop=(i == len(order) - 1))
+    mm.then_inc(S.mm, 1)
+
+    v.wait_ge(S.mm, 1)
+    v.tensor_copy(T.ys[:], T.acc[:]).then_inc(S.cp, 1)
+    g.sync.wait_ge(S.cp, 1)
+    g.sync.dma_start(T.y[:], T.ys[:]).then_inc(S.st, 16)
+    g.sync.wait_ge(S.st, 16)

@@ -7,6 +7,7 @@ D = 128
 
 SCRATCH = {
     "wd": ("dram", [D, D], "bfloat16"),
+    "rd": ("dram", [D, D], "bfloat16"),
     "W": ("sbuf", [D, NE * D], "bfloat16"),
     "xs": ("sbuf", [D, TOK], "bfloat16"),
     "mask": ("sbuf", [D, NE * TOK], "bfloat16"),
@@ -14,11 +15,18 @@ SCRATCH = {
     "acc": ("psum", [D, TOK], "float32"),
     "ys": ("sbuf", [D, TOK], "bfloat16"),
 }
-SEMAPHORES = ["ld", "h1", "sent", "xl", "mk", "xr", "mm", "cp", "st"] + ["ws%d" % j for j in range(NE)]
+SEMAPHORES = ["ld", "rl", "h1", "sent", "xl", "mk", "xr", "mm", "cp", "st"] + ["ws%d" % j for j in range(NE)]
 
 
 def _bits(m):
     return bin(m).count("1")
+
+
+def _and_mask(topo, src, dsts):
+    m = topo.mask(src, dsts[0])
+    for d in dsts:
+        m &= topo.mask(src, d)
+    return m
 
 
 def _plan(T, topo):
@@ -29,37 +37,74 @@ def _plan(T, topo):
     home = [cores[e] for e in experts]
     need = {c: sorted({slot[e] for tok in route[r] for e in tok}) for r, c in enumerate(cores)}
     chips = sorted({topo.chip(c) for c in cores})
+    mem = {k: [c for c in cores if topo.chip(c) == k] for k in chips}
+    flows = [(j, k) for j, h in enumerate(home) for k in chips
+             if k != topo.chip(h) and any(j in need[c] for c in mem[k])]
+
+    def cands(j, used):
+        h = home[j]
+        return [c for c in mem[topo.chip(h)] if c not in home and c not in used and topo.die(c) != topo.die(h)]
+
+    def load(rel):
+        ports = {}
+        for (j, k) in flows:
+            d = topo.die(rel.get((j, k), home[j]))
+            for p in ((0, topo.chip(home[j]), d), (1, k, d)):
+                ports[p] = ports.get(p, 0) + 1
+        return sorted(ports.values(), reverse=True)
+
+    rel = {}
+    history = [(load(rel), dict(rel))]
+    while True:
+        best = None
+        for f in flows:
+            if any(q[0] == f[0] for q in rel):
+                continue
+            cs = cands(f[0], list(rel.values()))
+            if cs:
+                trial = dict(rel)
+                trial[f] = cs[0]
+                if load(trial) < load(rel) and (best is None or load(trial) < load(best)):
+                    best = trial
+        if best is None:
+            break
+        rel = best
+        history.append((load(rel), dict(rel)))
+    low = min(h[0][0] for h in history)
+    rel = [h[1] for h in history if h[0][0] == low][0]
+
+    sender = {(k, j): rel.get((j, k), home[j]) for (j, k) in flows}
     spread = {}
-    for ch in chips:
-        mem = [c for c in cores if topo.chip(c) == ch]
-        free = [c for c in mem if c not in home]
-        foreign = []
+    for k in chips:
+        free = [c for c in mem[k] if c not in home]
         for j, h in enumerate(home):
-            if topo.chip(h) == ch:
-                spread[(ch, j)] = h
-            elif any(j in need[c] for c in mem):
-                foreign.append(j)
+            if topo.chip(h) == k:
+                spread[(k, j)] = h
+        foreign = [j for (j, kk) in flows if kk == k]
         for same_die in (True, False):
             for j in foreign:
-                if (ch, j) in spread:
+                if (k, j) in spread:
                     continue
                 for c in free:
-                    if topo.may_write(home[j], c) and (not same_die or topo.die(c) == topo.die(home[j])):
-                        spread[(ch, j)] = c
+                    if topo.may_write(sender[(k, j)], c) and (not same_die or topo.die(c) == topo.die(sender[(k, j)])):
+                        spread[(k, j)] = c
                         free.remove(c)
                         break
-    return cores, home, need, chips, spread
+    direct = {j: [spread[(k, j)] for (jj, k) in flows if jj == j and (j, k) not in rel] for j in range(len(home))}
+    relayed = {j: [(rel[(j, k)], spread[(k, j)]) for (jj, k) in flows if jj == j and (j, k) in rel]
+               for j in range(len(home))}
+    return cores, home, need, chips, spread, sender, direct, relayed
 
 
-def _send(g, topo, core, dsts, src, dst, rsem, lsem):
-    m = topo.mask(core, dsts[0])
-    for d in dsts:
-        m &= topo.mask(core, d)
+def _first_masks(topo, h, direct, relayed):
+    m_off = _and_mask(topo, h, direct) if direct else 0
+    m_rel = (topo.mask(h, relayed[0][0]) & ~m_off) if relayed else 0
+    return m_off, m_rel
+
+
+def _xfer(topo, dsts, m, src, dst, rsem):
     ids = [DstId(rid=topo.addr(d)[0], pnc=topo.addr(d)[1]) for d in dsts]
-    g.remote_dma_fused(
-        [RemoteDMATransfer(dst_ids=ids, dma_engine_mask=m, remote_sem=rsem, srcs=[src], dsts=[dst for _ in dsts])],
-        local_sem=lsem)
-    return _bits(m)
+    return RemoteDMATransfer(dst_ids=ids, dma_engine_mask=m, remote_sem=rsem, srcs=[src], dsts=[dst for _ in dsts])
 
 
 def rank_program(g, core, T, topo):
@@ -67,7 +112,7 @@ def rank_program(g, core, T, topo):
     if rank is None:
         return
     S = T.sem
-    cores, home, need, chips, spread = _plan(T, topo)
+    cores, home, need, chips, spread, sender, direct, relayed = _plan(T, topo)
     ch = topo.chip(core)
     mine = [j for j in range(NE) if spread.get((ch, j)) == core]
     my = mine[0] if mine else None
@@ -87,21 +132,36 @@ def rank_program(g, core, T, topo):
         g.scalar.dma_start(wblk(my), T.w[:]).then_inc(S["ws%d" % my], 16)
 
     sent = 0
+    for j in range(NE):
+        hops = [d for (r, d) in relayed[j] if r == core]
+        if hops:
+            g.wait_ge(S.rl, _bits(_first_masks(topo, home[j], direct[j], relayed[j])[1]))
+            m = _and_mask(topo, core, hops)
+            g.remote_dma_fused([_xfer(topo, hops, m, T.rd[:], T.wd[:], S.h1)], local_sem=S.sent)
+            sent += _bits(m)
     if my is not None:
         near = [c for c in cores if topo.chip(c) == ch and c != core and my in need[c]]
         if is_home:
             g.wait_ge(S.ld, 16)
-            far = [spread[(k, my)] for k in chips if k != ch and (k, my) in spread]
-            if far:
-                sent += _send(g, topo, core, far, T.wd[:], T.wd[:], S.h1, S.sent)
+            m_off, m_rel = _first_masks(topo, core, direct[my], relayed[my])
+            first = []
+            if direct[my]:
+                first.append(_xfer(topo, direct[my], m_off, T.wd[:], T.wd[:], S.h1))
+            if relayed[my]:
+                first.append(_xfer(topo, [relayed[my][0][0]], m_rel, T.wd[:], T.rd[:], S.rl))
+            if first:
+                g.remote_dma_fused(first, local_sem=S.sent)
+                sent += _bits(m_off) + _bits(m_rel)
         else:
-            n_in = _bits(topo.mask(home[my], core))
+            n_in = _bits(topo.mask(sender[(ch, my)], core))
             g.wait_ge(S.h1, n_in)
             if my in wants:
                 g.sync.wait_ge(S.h1, n_in)
                 g.sync.dma_start(wblk(my), T.wd[:]).then_inc(S["ws%d" % my], 16)
         if near:
-            sent += _send(g, topo, core, near, T.wd[:], wblk(my), S["ws%d" % my], S.sent)
+            m = _and_mask(topo, core, near)
+            g.remote_dma_fused([_xfer(topo, near, m, T.wd[:], wblk(my), S["ws%d" % my])], local_sem=S.sent)
+            sent += _bits(m)
     if sent:
         g.wait_ge(S.sent, sent)
 
@@ -126,7 +186,7 @@ def rank_program(g, core, T, topo):
 
     t = g.tensor
     t.wait_ge(S.xr, len(wants))
-    order = sorted(wants, key=lambda j: (topo.chip(home[j]) != ch, j != my, j))
+    order = sorted(wants, key=lambda j: (topo.chip(home[j]) != ch, sender.get((ch, j)) != home[j], j != my, j))
     for i, j in enumerate(order):
         src = spread[(ch, j)]
         t.wait_ge(S["ws%d" % j], 16 if src == core else _bits(topo.mask(src, core)))

from concourse.bass import DstId, RemoteDMATransfer
from concourse.mybir import AluOpType

NE = 8
TOK = 32
D = 128

SCRATCH = {
    "wd": ("dram", [D, D], "bfloat16"),
    "rd": ("dram", [D, D], "bfloat16"),
    "W": ("sbuf", [D, NE * D], "bfloat16"),
    "xs": ("sbuf", [D, TOK], "bfloat16"),
    "mask": ("sbuf", [D, NE * TOK], "bfloat16"),
    "xm": ("sbuf", [D, NE * TOK], "bfloat16"),
    "acc": ("psum", [D, TOK], "float32"),
    "ys": ("sbuf", [D, TOK], "bfloat16"),
}
SEMAPHORES = ["ld", "rl", "h1", "sent", "xl", "mk", "xr", "mm", "cp", "st"] + ["ws%d" % j for j in range(NE)]


def _bits(m):
    return bin(m).count("1")


def _and_mask(topo, src, dsts):
    m = topo.mask(src, dsts[0])
    for d in dsts:
        m &= topo.mask(src, d)
    return m


def _plan(T, topo):
    cores = list(T.cores)
    experts = list(T.tables["EXPERTS"])
    route = T.tables["ROUTE"]
    slot = {e: j for j, e in enumerate(experts)}
    home = [cores[e] for e in experts]
    need = {c: sorted({slot[e] for tok in route[r] for e in tok}) for r, c in enumerate(cores)}
    chips = sorted({topo.chip(c) for c in cores})
    mem = {k: [c for c in cores if topo.chip(c) == k] for k in chips}
    flows = [(j, k) for j, h in enumerate(home) for k in chips
             if k != topo.chip(h) and any(j in need[c] for c in mem[k])]

    def cands(j, used):
        h = home[j]
        return [c for c in mem[topo.chip(h)] if c not in home and c not in used and topo.die(c) != topo.die(h)]

    def load(rel):
        ports = {}
        for (j, k) in flows:
            d = topo.die(rel.get((j, k), home[j]))
            for p in ((0, topo.chip(home[j]), d), (1, k, d)):
                ports[p] = ports.get(p, 0) + 1
        return sorted(ports.values(), reverse=True)

    rel = {}
    history = [(load(rel), dict(rel))]
    while True:
        best = None
        for f in flows:
            if any(q[0] == f[0] for q in rel):
                continue
            cs = cands(f[0], list(rel.values()))
            if cs:
                trial = dict(rel)
                trial[f] = cs[0]
                if load(trial) < load(rel) and (best is None or load(trial) < load(best)):
                    best = trial
        if best is None:
            break
        rel = best
        history.append((load(rel), dict(rel)))
    low = min(h[0][0] for h in history)
    rel = [h[1] for h in history if h[0][0] == low][0]

    sender = {(k, j): rel.get((j, k), home[j]) for (j, k) in flows}
    spread = {}
    for k in chips:
        free = [c for c in mem[k] if c not in home]
        for j, h in enumerate(home):
            if topo.chip(h) == k:
                spread[(k, j)] = h
        foreign = [j for (j, kk) in flows if kk == k]
        for same_die in (True, False):
            for j in foreign:
                if (k, j) in spread:
                    continue
                for c in free:
                    if topo.may_write(sender[(k, j)], c) and (not same_die or topo.die(c) == topo.die(sender[(k, j)])):
                        spread[(k, j)] = c
                        free.remove(c)
                        break
    direct = {j: [spread[(k, j)] for (jj, k) in flows if jj == j and (j, k) not in rel] for j in range(len(home))}
    relayed = {j: [(rel[(j, k)], spread[(k, j)]) for (jj, k) in flows if jj == j and (j, k) in rel]
               for j in range(len(home))}
    return cores, home, need, chips, spread, sender, direct, relayed


def _first_masks(topo, h, direct, relayed):
    m_off = _and_mask(topo, h, direct) if direct else 0
    m_rel = (topo.mask(h, relayed[0][0]) & ~m_off) if relayed else 0
    return m_off, m_rel


def _xfer(topo, dsts, m, src, dst, rsem):
    ids = [DstId(rid=topo.addr(d)[0], pnc=topo.addr(d)[1]) for d in dsts]
    return RemoteDMATransfer(dst_ids=ids, dma_engine_mask=m, remote_sem=rsem, srcs=[src], dsts=[dst for _ in dsts])


def rank_program(g, core, T, topo):
    rank = T.rank_of(core)
    if rank is None:
        return
    S = T.sem
    cores, home, need, chips, spread, sender, direct, relayed = _plan(T, topo)
    ch = topo.chip(core)
    mine = [j for j in range(NE) if spread.get((ch, j)) == core]
    my = mine[0] if mine else None
    is_home = my is not None and home[my] == core
    wants = need[core]

    def wblk(j):
        return T.W[:, j * D:(j + 1) * D]

    def xblk(t, j):
        return t[:, j * TOK:(j + 1) * TOK]

    if is_home:
        g.sync.dma_start(T.wd[:], T.w[:]).then_inc(S.ld, 16)
    g.scalar.dma_start(T.xs[:], T.x[:]).then_inc(S.xl, 16)
    if is_home and my in wants:
        g.scalar.dma_start(wblk(my), T.w[:]).then_inc(S["ws%d" % my], 16)

    sent = 0
    for j in range(NE):
        hops = [d for (r, d) in relayed[j] if r == core]
        if hops:
            g.wait_ge(S.rl, _bits(_first_masks(topo, home[j], direct[j], relayed[j])[1]))
            m = _and_mask(topo, core, hops)
            g.remote_dma_fused([_xfer(topo, hops, m, T.rd[:], T.wd[:], S.h1)], local_sem=S.sent)
            sent += _bits(m)
    if my is not None:
        near = [c for c in cores if topo.chip(c) == ch and c != core and my in need[c]]
        if is_home:
            g.wait_ge(S.ld, 16)
            m_off, m_rel = _first_masks(topo, core, direct[my], relayed[my])
            first = []
            if direct[my]:
                first.append(_xfer(topo, direct[my], m_off, T.wd[:], T.wd[:], S.h1))
            if relayed[my]:
                first.append(_xfer(topo, [relayed[my][0][0]], m_rel, T.wd[:], T.rd[:], S.rl))
            if first:
                g.remote_dma_fused(first, local_sem=S.sent)
                sent += _bits(m_off) + _bits(m_rel)
        else:
            n_in = _bits(topo.mask(sender[(ch, my)], core))
            g.wait_ge(S.h1, n_in)
            if my in wants:
                g.sync.wait_ge(S.h1, n_in)
                g.sync.dma_start(wblk(my), T.wd[:]).then_inc(S["ws%d" % my], 16)
        if near:
            m = _and_mask(topo, core, near)
            g.remote_dma_fused([_xfer(topo, near, m, T.wd[:], wblk(my), S["ws%d" % my])], local_sem=S.sent)
            sent += _bits(m)
    if sent:
        g.wait_ge(S.sent, sent)

    v = g.vector
    v.memset(T.mask[:], 0.0).then_inc(S.mk, 1)
    v.wait_ge(S.mk, 1)
    nmk = 1
    experts = list(T.tables["EXPERTS"])
    cols = sorted(experts.index(e) * TOK + t for t, tok in enumerate(T.tables["ROUTE"][rank]) for e in tok)
    i = 0
    while i < len(cols):
        k = i
        while k + 1 < len(cols) and cols[k + 1] == cols[k] + 1:
            k += 1
        v.memset(T.mask[:, cols[i]:cols[k] + 1], 1.0).then_inc(S.mk, 1)
        nmk += 1
        i = k + 1
    v.wait_ge(S.mk, nmk)
    v.wait_ge(S.xl, 16)
    for j in wants:
        v.tensor_tensor(xblk(T.xm, j), T.xs[:], xblk(T.mask, j), AluOpType.mult).then_inc(S.xr, 1)

    t = g.tensor
    t.wait_ge(S.xr, len(wants))
    order = sorted(wants, key=lambda j: (topo.chip(home[j]) != ch, sender.get((ch, j)) != home[j], j != my, j))
    for i, j in enumerate(order):
        src = spread[(ch, j)]
        t.wait_ge(S["ws%d" % j], 16 if src == core else _bits(topo.mask(src, core)))
        mm = t.matmul(T.acc[:], wblk(j), xblk(T.xm, j), start=(i == 0), stop=(i == len(order) - 1))
    mm.then_inc(S.mm, 1)

    v.wait_ge(S.mm, 1)
    v.tensor_copy(T.ys[:], T.acc[:]).then_inc(S.cp, 1)
    g.sync.wait_ge(S.cp, 1)
    g.sync.dma_start(T.y[:], T.ys[:]).then_inc(S.st, 16)
    g.sync.wait_ge(S.st, 16)
